import numpy as np, ml_dtypes
CORES = [4,12,20,28,36,44,52,60,68,76,84,92,100,108,116,124,132,140,148,156,164,172,180,188,196,204,212,220,228,236,244,252]
N = 32
M, NO = 128, 256
def setup_inputs(rng):
    return {"a": rng.standard_normal((N, 128, N * M), dtype=np.float32).astype(ml_dtypes.bfloat16), "w": rng.standard_normal((N, 128, NO), dtype=np.float32).astype(ml_dtypes.bfloat16)}
def reference(a, w):
    tot = np.zeros((N * M, NO))
    for j in range(N):
        tot += a[j].astype(np.float64).T @ w[j].astype(np.float64)
    return {"y": np.stack([tot[r * M:(r + 1) * M] for r in range(N)]).astype(ml_dtypes.bfloat16 if a.dtype != np.float64 else np.float64)}

import concourse.bass as bass
from concourse.mybir import AluOpType

SCRATCH = {
    "tiles": ("sbuf", [128, 8, 768], "bfloat16"),
    "wbuf": ("sbuf", [128, 256], "bfloat16"),
    "recv": ("sbuf", [128, 4, 1280], "bfloat16"),
    "blocks": ("sbuf", [128, 8, 256], "bfloat16"),
    "acc": ("sbuf", [128, 2, 256], "float32"),
    "yout": ("sbuf", [128, 256], "bfloat16"),
    "ps": ("psum", [128, 4096], "float32"),
}
SEMAPHORES = ["in0", "in1", "in2", "in3", "in4", "in5", "in6", "in7", "loaded", "spread", "sent", "mm", "cp", "vs", "stored"]

RANK_CORE, WORK_CORE = 4, 2


def rank_program(g, core, T, topo):
    c = core % 8
    if c != RANK_CORE and c != WORK_CORE:
        return
    h, q = topo.host(core), topo.chip(core)
    t, u = q >> 2, q & 3
    e = 4 * h + u
    arrive = [T.sem.in0, T.sem.in1, T.sem.in2, T.sem.in3, T.sem.in4, T.sem.in5, T.sem.in6, T.sem.in7]

    def dst_id(hh, qq, cc):
        rid, pid = topo.addr(128 * hh + 8 * qq + cc, core)
        return bass.DstId(rid=rid, pnc=pid)

    if c == RANK_CORE:
        g.dma_start(T.tiles[:, :, 128:640], T.a[:, :]).then_inc(T.sem.loaded, 16)
        g.dma_start(T.wbuf[:, :], T.w[:, :]).then_inc(T.sem.loaded, 16)
        g.vector.wait_ge(T.sem.loaded, 32)
        for k in range(4):
            g.vector.tensor_copy(T.tiles[:, k, 640:768], T.wbuf[:, 0:128]).then_inc(T.sem.spread, 1)
            g.vector.tensor_copy(T.tiles[:, 4 + k, 0:128], T.wbuf[:, 128:256]).then_inc(T.sem.spread, 1)
        g.wait_ge(T.sem.spread, 8)
        step1 = []
        for n in range(4):
            k = (t + n) % 4
            for hh in range(2):
                step1.append(bass.RemoteDMATransfer(
                    dst_ids=[dst_id(h, 4 * k + u, WORK_CORE)],
                    dma_engine_mask=(0xF << (8 + 4 * hh) if n == 0 else 1 << (2 * (n - 1) + hh)),
                    remote_sem=arrive[t],
                    src=(T.tiles[:, k, 128:768] if hh == 0 else T.tiles[:, 4 + k, 0:640]),
                    dst=T.recv[:, t, 640 * hh:640 * hh + 640]))
        g.remote_dma_fused(step1, local_sem=T.sem.sent)
        order = [(e - n) % 8 for n in range(8)]
        g.vector.wait_ge(arrive[order[0]], 8)
        for n in range(1, 8):
            if n > 1:
                g.vector.wait_ge(T.sem.vs, n - 1)
            g.vector.wait_ge(arrive[order[n]], 1)
            g.vector.tensor_tensor(T.yout[:, :] if n == 7 else T.acc[:, (n + 1) % 2, :],
                                   T.blocks[:, order[0], :] if n == 1 else T.acc[:, n % 2, :],
                                   T.blocks[:, order[n], :], AluOpType.add).then_inc(T.sem.vs, 1)
        g.wait_ge(T.sem.vs, 7)
        g.dma_start(T.y[:, :], T.yout[:, :]).then_inc(T.sem.stored, 16)
        g.wait_ge(T.sem.stored, 16)
        g.wait_ge(T.sem.sent, 8 + 6)
        return

    dests = [(e + n) % 8 for n in range(8)]
    for n in range(4):
        s = (t - n) % 4
        g.tensor.wait_ge(arrive[s], 8 if n == 0 else 2)
        for i in dests:
            col = 768 * (i // 4) + 128 * (i % 4)
            mm = g.tensor.matmul(T.ps[:, 512 * i:512 * i + 256], T.recv[:, s, col:col + 128], T.recv[:, s, 512:768],
                                 n == 0, n == 3)
            if n == 3:
                mm.then_inc(T.sem.mm, 1)
    for n, i in enumerate(dests):
        g.vector.wait_ge(T.sem.mm, n + 1)
        g.vector.tensor_copy(T.blocks[:, i, :], T.ps[:, 512 * i:512 * i + 256]).then_inc(T.sem.cp, 1)
    g.wait_ge(T.sem.cp, 8)
    g.remote_dma_fused(
        [bass.RemoteDMATransfer(dst_ids=[dst_id(i // 4, 4 * t + i % 4, RANK_CORE)],
                                dma_engine_mask=(0xFF00 if n == 0 else 1 << (n - 1)),
                                remote_sem=arrive[e], src=T.blocks[:, i, :], dst=T.blocks[:, e, :])
         for n, i in enumerate(dests)],
        local_sem=T.sem.sent)
    g.wait_ge(T.sem.sent, 8 + 7)
